import numpy as np
CORES = [24,48,72,152,176,200]
N = 6
F = 128
def setup_inputs(rng):
    return {"x": rng.standard_normal((N, 128, N * F), dtype=np.float32), "w": rng.standard_normal((N, 128, 128), dtype=np.float32)}
def setup_inputs_big(rng):
    d = setup_inputs(rng)
    for k in ("x", "w"): d[k] = (d[k].astype(np.float32) * 1024.0).astype(d[k].dtype)
    return d
def setup_inputs_small(rng):
    d = setup_inputs(rng)
    for k in ("x", "w"): d[k] = (d[k].astype(np.float32) * (1 / 1024.0)).astype(d[k].dtype)
    return d
def setup_inputs_apart(rng):
    d = setup_inputs(rng)
    f = (10.0 ** rng.permutation(np.linspace(-1.5, 1.5, N))).astype(np.float32).reshape(N, 1, 1)
    for k in ("x", "w"): d[k] = (d[k].astype(np.float32) * f).astype(d[k].dtype)
    return d
def reference(x, w):
    X, W = x.astype(np.float64), w.astype(np.float64)
    s = X.sum(axis=0)
    o = np.concatenate([W[r].T @ s[:, F * r:F * r + F] for r in range(N)], axis=1).astype(np.float32 if x.dtype != np.float64 else np.float64)
    return {"y": np.broadcast_to(o, (N,) + o.shape)}

@@ -1,0 +1,181 @@
+from concourse.bass import DstId, RemoteDMATransfer
+
+N = 6
+F = 128
+
+SCRATCH = {
+    "xs": ("sbuf", [128, N * F], "float32"),
+    "ws": ("sbuf", [128, F], "float32"),
+    "land": ("sbuf", [128, N * F], "float32"),
+    "zs": ("sbuf", [128, F], "float32"),
+    "ps": ("psum", [128, F], "float32"),
+}
+SEMAPHORES = (["ld_a", "ld_b", "rl", "mm", "zr", "got_a", "got_b", "st_a", "st_b", "sent"]
+              + ["in%d" % j for j in range(N)])
+
+
+def _bits(mask):
+    return [e for e in range(mask.bit_length()) if (mask >> e) & 1]
+
+
+def _mask(engines):
+    m = 0
+    for e in engines:
+        m |= 1 << e
+    return m
+
+
+def _split(engines, k):
+    if k == 1:
+        return [engines]
+    return _split(engines[0::2], k // 2) + _split(engines[1::2], k - k // 2)
+
+
+def _blk(t, r):
+    return t[:, r * F:(r + 1) * F]
+
+
+def _plan(T, topo):
+    ranks = list(T.cores)
+    p = {"ranks": ranks, "direct": [], "cross": [], "relay": [], "H": [], "place": []}
+    for i, c in enumerate(ranks):
+        others = [r for r in range(N) if r != i]
+        direct = [r for r in others if topo.may_write(c, ranks[r])]
+        cross = [r for r in others if not topo.may_write(c, ranks[r])]
+        chipmates = [d for d in range(c - topo.CORES_PER_CHIP, c + topo.CORES_PER_CHIP)
+                     if d != c and d >= 0 and topo.host(d) == topo.host(c) and topo.chip(d) == topo.chip(c)]
+        owners = [d for d in chipmates if all(topo.may_write(d, ranks[r]) for r in others)]
+        near = [d for d in owners if topo.die(d) == topo.die(c)]
+        far = [d for d in owners if topo.die(d) != topo.die(c)]
+        seq = []
+        for a, b in zip(near, far):
+            seq += [a, b]
+        place = sorted(direct + [i]).index(i)
+        m = len(cross)
+        p["direct"].append(direct)
+        p["cross"].append(cross)
+        p["place"].append(place)
+        p["relay"].append({r: seq[(q + place) % m] for q, r in enumerate(cross)})
+        p["H"].append(seq[place % 2])
+    return p
+
+
+def _rank_calls(p, i, topo):
+    c = p["ranks"][i]
+    h = p["H"][i]
+    on = _bits(topo.mask(c, h))
+    off = on
+    for r in p["direct"][i]:
+        off = [e for e in off if e in _bits(topo.mask(c, p["H"][r]))]
+    extra = [e for e in on if e not in off]
+    jobs = sorted(p["relay"][i].items(), key=lambda rd: (topo.die(rd[1]) != topo.die(c), rd[0]))
+    pool = extra if 4 * len(jobs) <= len(extra) else on
+    first = [("x", r, d, e) for (r, d), e in zip(jobs, _split(pool, len(jobs)))]
+    second = [("x", r, p["H"][r], e) for r, e in zip(p["direct"][i], _split(off, len(p["direct"][i])))]
+    own = _split(extra, 2)
+    second += [("x", i, h, own[0]), ("w", i, h, own[1])]
+    return first, second
+
+
+def rank_program(g, core, T, topo):
+    p = _plan(T, topo)
+    ranks, H = p["ranks"], p["H"]
+    calls = [_rank_calls(p, j, topo) for j in range(N)]
+    half = N // 2
+    got = lambda r: T.sem.got_a if r < half else T.sem.got_b
+    back_on = lambda r: _split([e for e in _bits(topo.mask(H[r], ranks[r]))
+                                if e not in _bits(topo.mask(H[r], ranks[(r + 1) % N]))], 2)[0]
+    back_off = lambda r: _bits(min(topo.mask(H[r], ranks[d]) for d in range(N) if d != r))
+
+    def dst_id(d):
+        rid, pid = topo.addr(d, core)
+        return DstId(rid=rid, pnc=pid)
+
+    i = T.rank_of(core)
+    if i is not None:
+        crit = sorted(p["cross"][i])
+        if 2 * len(crit) > N:
+            runs_a, rest = [(0, half), (half, N)], []
+        else:
+            runs_a, rest = [(r, r + 1) for r in crit], [r for r in range(N) if r not in crit]
+        runs_b = []
+        for r in rest:
+            if runs_b and runs_b[-1][1] == r:
+                runs_b[-1] = (runs_b[-1][0], r + 1)
+            else:
+                runs_b.append((r, r + 1))
+        runs_b.sort(key=lambda ab: ab[0] - ab[1])
+        queues = [g.sync, g.scalar]
+        load = [0, 0]
+        for sem, runs in ((T.sem.ld_a, runs_a), (T.sem.ld_b, runs_b + [None])):
+            for run in runs:
+                k = 0 if load[0] <= load[1] else 1
+                if run is None:
+                    queues[k].dma_start(T.ws[:], T.w[:]).then_inc(sem, 16)
+                    load[k] += 1
+                else:
+                    a, b = run
+                    queues[k].dma_start(T.xs[:, a * F:b * F], T.x[:, a * F:b * F]).then_inc(sem, 16)
+                    load[k] += b - a
+        sent = 0
+        for sem, n_dma, call in ((T.sem.ld_a, len(runs_a), calls[i][0]), (T.sem.ld_b, len(runs_b) + 1, calls[i][1])):
+            g.wait_ge(sem, 16 * n_dma)
+            trs = []
+            for what, r, d, eng in call:
+                if what == "w":
+                    src, dst, rs = T.ws[:], T.ws[:], T.sem["in%d" % i]
+                elif d == H[r]:
+                    src, dst, rs = _blk(T.xs, r), _blk(T.land, i), T.sem["in%d" % i]
+                else:
+                    src, dst, rs = _blk(T.xs, r), _blk(T.xs, r), T.sem.rl
+                trs.append(RemoteDMATransfer(dst_ids=[dst_id(d)], dma_engine_mask=_mask(eng), remote_sem=rs,
+                                             src=src, dst=dst))
+                sent += len(eng)
+            g.remote_dma_fused(trs, local_sem=T.sem.sent)
+        for q, lo, hi, gs, ss in ((g.sync, 0, half, T.sem.got_a, T.sem.st_a), (g.scalar, half, N, T.sem.got_b, T.sem.st_b)):
+            q.wait_ge(gs, sum(len(back_on(r)) if r == i else len(back_off(r)) for r in range(lo, hi)))
+            q.dma_start(T.y[:, lo * F:hi * F], T.land[:, lo * F:hi * F]).then_inc(ss, 16)
+            q.wait_ge(ss, 16)
+        g.wait_ge(T.sem.sent, sent)
+        return
+
+    sent = 0
+    for j in range(N):
+        for what, r, d, eng in calls[j][0]:
+            if d == core:
+                g.wait_ge(T.sem.rl, len(eng))
+                rid, pid = topo.addr(H[r], core)
+                m = topo.mask(core, H[r])
+                g.remote_dma(out_ap=_blk(T.land, j), in_ap=_blk(T.xs, r), remote_sem=T.sem["in%d" % j],
+                             local_sem=T.sem.sent, pid=pid, routing_id=rid, dma_engine_mask=m)
+                sent += len(_bits(m))
+
+    if core in H:
+        r = H.index(core)
+        order = [r] + p["direct"][r] + p["cross"][r]
+        for k, j in enumerate(order):
+            if j == r:
+                n_in = sum(len(e) for _, _, d, e in calls[r][1] if d == core)
+            elif j in p["direct"][r]:
+                n_in = sum(len(e) for _, b, d, e in calls[j][1] if d == core)
+            else:
+                n_in = len(_bits(topo.mask(p["relay"][j][r], core)))
+            g.tensor.wait_ge(T.sem["in%d" % j], n_in)
+            mm = g.tensor.matmul(T.ps[:], T.ws[:], _blk(T.land, j), start=(k == 0), stop=(k == N - 1))
+        mm.then_inc(T.sem.mm, 1)
+        g.vector.wait_ge(T.sem.mm, 1)
+        g.vector.tensor_copy(T.zs[:], T.ps[:]).then_inc(T.sem.zr, 1)
+        g.wait_ge(T.sem.zr, 1)
+        away = [(r + k) % N for k in range(1, N)]
+        eng = back_off(r)
+        g.remote_dma_fused([RemoteDMATransfer(dst_ids=[dst_id(ranks[d]) for d in away], dma_engine_mask=_mask(eng),
+                                              remote_sem=got(r), srcs=[T.zs[:]], dsts=[_blk(T.land, r) for d in away])],
+                           local_sem=T.sem.sent)
+        sent += len(eng)
+        rid, pid = topo.addr(ranks[r], core)
+        eng = back_on(r)
+        g.remote_dma(out_ap=_blk(T.land, r), in_ap=T.zs[:], remote_sem=got(r), local_sem=T.sem.sent, pid=pid,
+                     routing_id=rid, dma_engine_mask=_mask(eng))
+        sent += len(eng)
+    if sent:
+        g.wait_ge(T.sem.sent, sent)

@@ -2,16 +2,18 @@ from concourse.bass import DstId, RemoteDMATransfer
 
 N = 6
 F = 128
+HF = F // 2
+STORE_GROUP = 3
 
 SCRATCH = {
     "xs": ("sbuf", [128, N * F], "float32"),
     "ws": ("sbuf", [128, F], "float32"),
     "land": ("sbuf", [128, N * F], "float32"),
-    "zs": ("sbuf", [128, F], "float32"),
-    "ps": ("psum", [128, F], "float32"),
+    "zs": ("sbuf", [128, HF], "float32"),
+    "ps": ("psum", [128, HF], "float32"),
 }
-SEMAPHORES = (["ld_a", "ld_b", "rl", "mm", "zr", "got_a", "got_b", "st_a", "st_b", "sent"]
-              + ["in%d" % j for j in range(N)])
+SEMAPHORES = (["ld_a", "ld_b", "ld_w", "rl", "mm", "zr", "st_a", "st_b", "sent"]
+              + ["in%d" % j for j in range(N)] + ["got%d" % j for j in range(N // STORE_GROUP)])
 
 
 def _bits(mask):
@@ -35,9 +37,13 @@ def _blk(t, r):
     return t[:, r * F:(r + 1) * F]
 
 
+def _hlf(t, r, h):
+    return t[:, r * F + h * HF:r * F + (h + 1) * HF]
+
+
 def _plan(T, topo):
     ranks = list(T.cores)
-    p = {"ranks": ranks, "direct": [], "cross": [], "relay": [], "H": [], "place": []}
+    p = {"ranks": ranks, "direct": [], "cross": [], "relay": [], "H": []}
     for i, c in enumerate(ranks):
         others = [r for r in range(N) if r != i]
         direct = [r for r in others if topo.may_write(c, ranks[r])]
@@ -54,27 +60,27 @@ def _plan(T, topo):
         m = len(cross)
         p["direct"].append(direct)
         p["cross"].append(cross)
-        p["place"].append(place)
         p["relay"].append({r: seq[(q + place) % m] for q, r in enumerate(cross)})
-        p["H"].append(seq[place % 2])
+        p["H"].append(seq[0:2])
     return p
 
 
 def _rank_calls(p, i, topo):
     c = p["ranks"][i]
-    h = p["H"][i]
-    on = _bits(topo.mask(c, h))
+    hs = p["H"][i]
+    on = _bits(topo.mask(c, hs[0]))
     off = on
     for r in p["direct"][i]:
-        off = [e for e in off if e in _bits(topo.mask(c, p["H"][r]))]
+        off = [e for e in off if e in _bits(topo.mask(c, p["H"][r][0]))]
     extra = [e for e in on if e not in off]
     jobs = sorted(p["relay"][i].items(), key=lambda rd: (topo.die(rd[1]) != topo.die(c), rd[0]))
-    pool = extra if 4 * len(jobs) <= len(extra) else on
-    first = [("x", r, d, e) for (r, d), e in zip(jobs, _split(pool, len(jobs)))]
-    second = [("x", r, p["H"][r], e) for r, e in zip(p["direct"][i], _split(off, len(p["direct"][i])))]
-    own = _split(extra, 2)
-    second += [("x", i, h, own[0]), ("w", i, h, own[1])]
-    return first, second
+    pool = on if 4 * len(jobs) > len(extra) else extra
+    first = [("x", r, None, d, e) for (r, d), e in zip(jobs, _split(pool, len(jobs)))]
+    away = [(r, h) for h in range(2) for r in p["direct"][i]]
+    second = [("x", r, h, p["H"][r][h], e) for (r, h), e in zip(away, _split(off, len(away)))]
+    second += [("x", i, h, hs[h], e) for h, e in zip(range(2), _split(extra, 2))]
+    third = [("w", i, None, hs[h], e) for h, e in zip(range(2), _split(extra, 2))]
+    return first, second, third
 
 
 def rank_program(g, core, T, topo):
@@ -82,10 +88,10 @@ def rank_program(g, core, T, topo):
     ranks, H = p["ranks"], p["H"]
     calls = [_rank_calls(p, j, topo) for j in range(N)]
     half = N // 2
-    got = lambda r: T.sem.got_a if r < half else T.sem.got_b
-    back_on = lambda r: _split([e for e in _bits(topo.mask(H[r], ranks[r]))
-                                if e not in _bits(topo.mask(H[r], ranks[(r + 1) % N]))], 2)[0]
-    back_off = lambda r: _bits(min(topo.mask(H[r], ranks[d]) for d in range(N) if d != r))
+    got = lambda r: T.sem["got%d" % (r // STORE_GROUP)]
+    back_on = lambda r, h: _split([e for e in _bits(topo.mask(H[r][h], ranks[r]))
+                                   if e not in _bits(topo.mask(H[r][h], ranks[(r + 1) % N]))], 2)[0]
+    back_off = lambda r, h: _bits(min(topo.mask(H[r][h], ranks[d]) for d in range(N) if d != r))
 
     def dst_id(d):
         rid, pid = topo.addr(d, core)
@@ -107,7 +113,7 @@ def rank_program(g, core, T, topo):
         runs_b.sort(key=lambda ab: ab[0] - ab[1])
         queues = [g.sync, g.scalar]
         load = [0, 0]
-        for sem, runs in ((T.sem.ld_a, runs_a), (T.sem.ld_b, runs_b + [None])):
+        for sem, runs in ((T.sem.ld_a, runs_a), (T.sem.ld_b, runs_b), (T.sem.ld_w, [None])):
             for run in runs:
                 k = 0 if load[0] <= load[1] else 1
                 if run is None:
@@ -118,63 +124,68 @@ def rank_program(g, core, T, topo):
                     queues[k].dma_start(T.xs[:, a * F:b * F], T.x[:, a * F:b * F]).then_inc(sem, 16)
                     load[k] += b - a
         sent = 0
-        for sem, n_dma, call in ((T.sem.ld_a, len(runs_a), calls[i][0]), (T.sem.ld_b, len(runs_b) + 1, calls[i][1])):
-            g.wait_ge(sem, 16 * n_dma)
+        for sem, n_dma, call in ((T.sem.ld_a, len(runs_a), calls[i][0]), (T.sem.ld_b, len(runs_b), calls[i][1]),
+                                 (T.sem.ld_w, 1, calls[i][2])):
+            if n_dma:
+                g.wait_ge(sem, 16 * n_dma)
             trs = []
-            for what, r, d, eng in call:
+            for what, r, h, d, eng in call:
                 if what == "w":
                     src, dst, rs = T.ws[:], T.ws[:], T.sem["in%d" % i]
-                elif d == H[r]:
-                    src, dst, rs = _blk(T.xs, r), _blk(T.land, i), T.sem["in%d" % i]
-                else:
+                elif h is None:
                     src, dst, rs = _blk(T.xs, r), _blk(T.xs, r), T.sem.rl
+                else:
+                    src, dst, rs = _hlf(T.xs, r, h), _hlf(T.land, i, h), T.sem["in%d" % i]
                 trs.append(RemoteDMATransfer(dst_ids=[dst_id(d)], dma_engine_mask=_mask(eng), remote_sem=rs,
                                              src=src, dst=dst))
                 sent += len(eng)
             g.remote_dma_fused(trs, local_sem=T.sem.sent)
-        for q, lo, hi, gs, ss in ((g.sync, 0, half, T.sem.got_a, T.sem.st_a), (g.scalar, half, N, T.sem.got_b, T.sem.st_b)):
-            q.wait_ge(gs, sum(len(back_on(r)) if r == i else len(back_off(r)) for r in range(lo, hi)))
-            q.dma_start(T.y[:, lo * F:hi * F], T.land[:, lo * F:hi * F]).then_inc(ss, 16)
-            q.wait_ge(ss, 16)
+        groups = [list(range(a, a + STORE_GROUP)) for a in range(0, N, STORE_GROUP)]
+        groups.sort(key=lambda rs: max((i - r) % N for r in rs))
+        for q, ss, mine in ((g.sync, T.sem.st_a, groups[0::2]), (g.scalar, T.sem.st_b, groups[1::2])):
+            for rs in mine:
+                q.wait_ge(got(rs[0]), sum(len(back_on(r, h)) if r == i else len(back_off(r, h))
+                                          for r in rs for h in range(2)))
+                q.dma_start(T.y[:, rs[0] * F:(rs[-1] + 1) * F], T.land[:, rs[0] * F:(rs[-1] + 1) * F]).then_inc(ss, 16)
+            q.wait_ge(ss, 16 * len(mine))
         g.wait_ge(T.sem.sent, sent)
         return
 
+    relay_eng = lambda d, r: _split(_bits(min(topo.mask(d, H[r][h]) for h in range(2))), 2)
     sent = 0
     for j in range(N):
-        for what, r, d, eng in calls[j][0]:
+        for what, r, _h, d, eng in calls[j][0]:
             if d == core:
                 g.wait_ge(T.sem.rl, len(eng))
-                rid, pid = topo.addr(H[r], core)
-                m = topo.mask(core, H[r])
-                g.remote_dma(out_ap=_blk(T.land, j), in_ap=_blk(T.xs, r), remote_sem=T.sem["in%d" % j],
-                             local_sem=T.sem.sent, pid=pid, routing_id=rid, dma_engine_mask=m)
-                sent += len(_bits(m))
+                es = relay_eng(core, r)
+                g.remote_dma_fused([RemoteDMATransfer(dst_ids=[dst_id(H[r][h])], dma_engine_mask=_mask(es[h]),
+                                                      remote_sem=T.sem["in%d" % j], src=_hlf(T.xs, r, h),
+                                                      dst=_hlf(T.land, j, h)) for h in range(2)], local_sem=T.sem.sent)
+                sent += sum(len(e) for e in es)
 
-    if core in H:
-        r = H.index(core)
+    mine = [(r, h) for r in range(N) for h in range(2) if H[r][h] == core]
+    for r, h in mine:
         order = [r] + p["direct"][r] + p["cross"][r]
         for k, j in enumerate(order):
-            if j == r:
-                n_in = sum(len(e) for _, _, d, e in calls[r][1] if d == core)
-            elif j in p["direct"][r]:
-                n_in = sum(len(e) for _, b, d, e in calls[j][1] if d == core)
+            if j in p["cross"][r]:
+                n_in = len(relay_eng(p["relay"][j][r], r)[h])
             else:
-                n_in = len(_bits(topo.mask(p["relay"][j][r], core)))
+                n_in = sum(len(e) for call in calls[j][1:] for _, _, _, d, e in call if d == core)
             g.tensor.wait_ge(T.sem["in%d" % j], n_in)
-            mm = g.tensor.matmul(T.ps[:], T.ws[:], _blk(T.land, j), start=(k == 0), stop=(k == N - 1))
+            mm = g.tensor.matmul(T.ps[:], T.ws[:], _hlf(T.land, j, h), start=(k == 0), stop=(k == N - 1))
         mm.then_inc(T.sem.mm, 1)
         g.vector.wait_ge(T.sem.mm, 1)
         g.vector.tensor_copy(T.zs[:], T.ps[:]).then_inc(T.sem.zr, 1)
         g.wait_ge(T.sem.zr, 1)
         away = [(r + k) % N for k in range(1, N)]
-        eng = back_off(r)
+        eng = back_off(r, h)
         g.remote_dma_fused([RemoteDMATransfer(dst_ids=[dst_id(ranks[d]) for d in away], dma_engine_mask=_mask(eng),
-                                              remote_sem=got(r), srcs=[T.zs[:]], dsts=[_blk(T.land, r) for d in away])],
+                                              remote_sem=got(r), srcs=[T.zs[:]], dsts=[_hlf(T.land, r, h) for d in away])],
                            local_sem=T.sem.sent)
         sent += len(eng)
         rid, pid = topo.addr(ranks[r], core)
-        eng = back_on(r)
-        g.remote_dma(out_ap=_blk(T.land, r), in_ap=T.zs[:], remote_sem=got(r), local_sem=T.sem.sent, pid=pid,
+        eng = back_on(r, h)
+        g.remote_dma(out_ap=_hlf(T.land, r, h), in_ap=T.zs[:], remote_sem=got(r), local_sem=T.sem.sent, pid=pid,
                      routing_id=rid, dma_engine_mask=_mask(eng))
         sent += len(eng)
     if sent:

@@ -3,7 +3,6 @@ from concourse.bass import DstId, RemoteDMATransfer
 N = 6
 F = 128
 HF = F // 2
-STORE_GROUP = 3
 
 SCRATCH = {
     "xs": ("sbuf", [128, N * F], "float32"),
@@ -12,8 +11,8 @@ SCRATCH = {
     "zs": ("sbuf", [128, HF], "float32"),
     "ps": ("psum", [128, HF], "float32"),
 }
-SEMAPHORES = (["ld_a", "ld_b", "ld_w", "rl", "mm", "zr", "st_a", "st_b", "sent"]
-              + ["in%d" % j for j in range(N)] + ["got%d" % j for j in range(N // STORE_GROUP)])
+SEMAPHORES = (["ld_a0", "ld_a1", "ld_b", "ld_w", "rl", "inw", "mm", "zr", "st_a", "st_b", "sent"]
+              + ["in%d" % j for j in range(N)] + ["got%d" % j for j in range(N)])
 
 
 def _bits(mask):
@@ -33,6 +32,17 @@ def _split(engines, k):
     return _split(engines[0::2], k // 2) + _split(engines[1::2], k - k // 2)
 
 
+def _runs(blocks):
+    runs = []
+    for r in sorted(blocks):
+        if runs and runs[-1][1] == r:
+            runs[-1] = (runs[-1][0], r + 1)
+        else:
+            runs.append((r, r + 1))
+    runs.sort(key=lambda ab: ab[0] - ab[1])
+    return runs
+
+
 def _blk(t, r):
     return t[:, r * F:(r + 1) * F]
 
@@ -43,7 +53,7 @@ def _hlf(t, r, h):
 
 def _plan(T, topo):
     ranks = list(T.cores)
-    p = {"ranks": ranks, "direct": [], "cross": [], "relay": [], "H": []}
+    p = {"ranks": ranks, "direct": [], "cross": [], "relay": [], "H": [], "waves": [], "late": []}
     for i, c in enumerate(ranks):
         others = [r for r in range(N) if r != i]
         direct = [r for r in others if topo.may_write(c, ranks[r])]
@@ -62,6 +72,12 @@ def _plan(T, topo):
         p["cross"].append(cross)
         p["relay"].append({r: seq[(q + place) % m] for q, r in enumerate(cross)})
         p["H"].append(seq[0:2])
+        inner = cross[m // 4:m // 4 + m // 2]
+        outer = [r for r in cross if r not in inner]
+        k = (2 * place // (len(direct) + 1)) % 2
+        p["waves"].append([inner, outer] if k == 0 else [outer, inner])
+        plane = sorted(direct + [i])
+        p["late"].append(plane[(place + 1) % len(plane)])
     return p
 
 
@@ -73,22 +89,32 @@ def _rank_calls(p, i, topo):
     for r in p["direct"][i]:
         off = [e for e in off if e in _bits(topo.mask(c, p["H"][r][0]))]
     extra = [e for e in on if e not in off]
-    jobs = sorted(p["relay"][i].items(), key=lambda rd: (topo.die(rd[1]) != topo.die(c), rd[0]))
-    pool = on if 4 * len(jobs) > len(extra) else extra
-    first = [("x", r, None, d, e) for (r, d), e in zip(jobs, _split(pool, len(jobs)))]
-    away = [(r, h) for h in range(2) for r in p["direct"][i]]
-    second = [("x", r, h, p["H"][r][h], e) for (r, h), e in zip(away, _split(off, len(away)))]
-    second += [("x", i, h, hs[h], e) for h, e in zip(range(2), _split(extra, 2))]
-    third = [("w", i, None, hs[h], e) for h, e in zip(range(2), _split(extra, 2))]
-    return first, second, third
+    pool = on if 4 * len(p["cross"][i]) > len(extra) else extra
+    waves = []
+    for wave in p["waves"][i]:
+        jobs = sorted([(r, p["relay"][i][r]) for r in wave], key=lambda rd: (topo.die(rd[1]) != topo.die(c), rd[0]))
+        waves.append([("x", r, None, d, e) for (r, d), e in zip(jobs, _split(pool, len(jobs)))])
+    dl = [r for r in p["direct"][i] if r != p["late"][i]] + [p["late"][i]]
+    away = [(r, h) for r in dl for h in range(2)]
+    n1 = 1
+    while 2 * n1 <= len(away):
+        n1 *= 2
+    first = [("x", r, h, p["H"][r][h], e) for (r, h), e in zip(away[:n1], _split(off, n1))]
+    own = [("x", i, h, hs[h], e) for h, e in zip(range(2), _split(extra, 2))]
+    if n1 < len(away):
+        more = [("x", r, h, p["H"][r][h], e) for (r, h), e in zip(away[n1:], _split(off, len(away) - n1))]
+        wh = [("wh", i, k, hs[h], e) for (k, h), e in zip([(k, h) for k in range(2) for h in range(2)], _split(extra, 4))]
+        rest = [(["ld_w", "ld_b"], first + wh), ([], more + own)]
+    else:
+        rest = [(["ld_w"], [("w", i, None, hs[h], e) for h, e in zip(range(2), _split(extra, 2))]), (["ld_b"], first + own)]
+    return {"waves": waves, "rest": rest}
 
 
 def rank_program(g, core, T, topo):
     p = _plan(T, topo)
     ranks, H = p["ranks"], p["H"]
     calls = [_rank_calls(p, j, topo) for j in range(N)]
-    half = N // 2
-    got = lambda r: T.sem["got%d" % (r // STORE_GROUP)]
+    got = lambda r: T.sem["got%d" % r]
     back_on = lambda r, h: _split([e for e in _bits(topo.mask(H[r][h], ranks[r]))
                                    if e not in _bits(topo.mask(H[r][h], ranks[(r + 1) % N]))], 2)[0]
     back_off = lambda r, h: _bits(min(topo.mask(H[r][h], ranks[d]) for d in range(N) if d != r))
@@ -99,39 +125,30 @@ def rank_program(g, core, T, topo):
 
     i = T.rank_of(core)
     if i is not None:
-        crit = sorted(p["cross"][i])
-        if 2 * len(crit) > N:
-            runs_a, rest = [(0, half), (half, N)], []
-        else:
-            runs_a, rest = [(r, r + 1) for r in crit], [r for r in range(N) if r not in crit]
-        runs_b = []
-        for r in rest:
-            if runs_b and runs_b[-1][1] == r:
-                runs_b[-1] = (runs_b[-1][0], r + 1)
-            else:
-                runs_b.append((r, r + 1))
-        runs_b.sort(key=lambda ab: ab[0] - ab[1])
+        rest = [r for r in range(N) if r not in p["cross"][i]]
+        loads = {"ld_a0": _runs(p["waves"][i][0]), "ld_a1": _runs(p["waves"][i][1]), "ld_w": [None], "ld_b": _runs(rest)}
         queues = [g.sync, g.scalar]
         load = [0, 0]
-        for sem, runs in ((T.sem.ld_a, runs_a), (T.sem.ld_b, runs_b), (T.sem.ld_w, [None])):
-            for run in runs:
+        for name in ("ld_a0", "ld_a1", "ld_w", "ld_b"):
+            for run in loads[name]:
                 k = 0 if load[0] <= load[1] else 1
                 if run is None:
-                    queues[k].dma_start(T.ws[:], T.w[:]).then_inc(sem, 16)
+                    queues[k].dma_start(T.ws[:], T.w[:]).then_inc(T.sem[name], 16)
                     load[k] += 1
                 else:
                     a, b = run
-                    queues[k].dma_start(T.xs[:, a * F:b * F], T.x[:, a * F:b * F]).then_inc(sem, 16)
+                    queues[k].dma_start(T.xs[:, a * F:b * F], T.x[:, a * F:b * F]).then_inc(T.sem[name], 16)
                     load[k] += b - a
         sent = 0
-        for sem, n_dma, call in ((T.sem.ld_a, len(runs_a), calls[i][0]), (T.sem.ld_b, len(runs_b), calls[i][1]),
-                                 (T.sem.ld_w, 1, calls[i][2])):
-            if n_dma:
-                g.wait_ge(sem, 16 * n_dma)
+        for names, call in [(["ld_a0"], calls[i]["waves"][0]), (["ld_a1"], calls[i]["waves"][1])] + calls[i]["rest"]:
+            for name in names:
+                g.wait_ge(T.sem[name], 16 * len(loads[name]))
             trs = []
             for what, r, h, d, eng in call:
                 if what == "w":
-                    src, dst, rs = T.ws[:], T.ws[:], T.sem["in%d" % i]
+                    src, dst, rs = T.ws[:], T.ws[:], T.sem.inw
+                elif what == "wh":
+                    src, dst, rs = _hlf(T.ws, 0, h), _hlf(T.ws, 0, h), T.sem.inw
                 elif h is None:
                     src, dst, rs = _blk(T.xs, r), _blk(T.xs, r), T.sem.rl
                 else:
@@ -140,13 +157,11 @@ def rank_program(g, core, T, topo):
                                              src=src, dst=dst))
                 sent += len(eng)
             g.remote_dma_fused(trs, local_sem=T.sem.sent)
-        groups = [list(range(a, a + STORE_GROUP)) for a in range(0, N, STORE_GROUP)]
-        groups.sort(key=lambda rs: max((i - r) % N for r in rs))
-        for q, ss, mine in ((g.sync, T.sem.st_a, groups[0::2]), (g.scalar, T.sem.st_b, groups[1::2])):
-            for rs in mine:
-                q.wait_ge(got(rs[0]), sum(len(back_on(r, h)) if r == i else len(back_off(r, h))
-                                          for r in rs for h in range(2)))
-                q.dma_start(T.y[:, rs[0] * F:(rs[-1] + 1) * F], T.land[:, rs[0] * F:(rs[-1] + 1) * F]).then_inc(ss, 16)
+        turn = sorted(range(N), key=lambda r: (i - r) % N)
+        for q, ss, mine in ((g.sync, T.sem.st_a, turn[0::2]), (g.scalar, T.sem.st_b, turn[1::2])):
+            for r in mine:
+                q.wait_ge(got(r), sum(len(back_on(r, h)) if r == i else len(back_off(r, h)) for h in range(2)))
+                q.dma_start(_blk(T.y, r), _blk(T.land, r)).then_inc(ss, 16)
             q.wait_ge(ss, 16 * len(mine))
         g.wait_ge(T.sem.sent, sent)
         return
@@ -154,23 +169,31 @@ def rank_program(g, core, T, topo):
     relay_eng = lambda d, r: _split(_bits(min(topo.mask(d, H[r][h]) for h in range(2))), 2)
     sent = 0
     for j in range(N):
-        for what, r, _h, d, eng in calls[j][0]:
-            if d == core:
-                g.wait_ge(T.sem.rl, len(eng))
-                es = relay_eng(core, r)
-                g.remote_dma_fused([RemoteDMATransfer(dst_ids=[dst_id(H[r][h])], dma_engine_mask=_mask(es[h]),
-                                                      remote_sem=T.sem["in%d" % j], src=_hlf(T.xs, r, h),
-                                                      dst=_hlf(T.land, j, h)) for h in range(2)], local_sem=T.sem.sent)
-                sent += sum(len(e) for e in es)
+        for call in calls[j]["waves"]:
+            for what, r, _h, d, eng in call:
+                if d == core:
+                    g.wait_ge(T.sem.rl, len(eng))
+                    es = relay_eng(core, r)
+                    g.remote_dma_fused([RemoteDMATransfer(dst_ids=[dst_id(H[r][h])], dma_engine_mask=_mask(es[h]),
+                                                          remote_sem=T.sem["in%d" % j], src=_hlf(T.xs, r, h),
+                                                          dst=_hlf(T.land, j, h)) for h in range(2)],
+                                       local_sem=T.sem.sent)
+                    sent += sum(len(e) for e in es)
 
     mine = [(r, h) for r in range(N) for h in range(2) if H[r][h] == core]
     for r, h in mine:
-        order = [r] + p["direct"][r] + p["cross"][r]
+        two = lambda j: any(w == "wh" for _, call in calls[j]["rest"] for w, _, _, _, _ in call)
+        last = [j for j in p["direct"][r] if two(j) and p["late"][j] == r]
+        soon = [j for j in p["direct"][r] if j not in last]
+        order = ((soon + [r] if two(r) else [r] + soon) + [j for j in p["cross"][r] if r in p["waves"][j][0]]
+                 + last + [j for j in p["cross"][r] if r not in p["waves"][j][0]])
+        g.tensor.wait_ge(T.sem.inw, sum(len(e) for _, call in calls[r]["rest"] for w, _, _, d, e in call
+                                        if w != "x" and d == core))
         for k, j in enumerate(order):
             if j in p["cross"][r]:
                 n_in = len(relay_eng(p["relay"][j][r], r)[h])
             else:
-                n_in = sum(len(e) for call in calls[j][1:] for _, _, _, d, e in call if d == core)
+                n_in = sum(len(e) for _, call in calls[j]["rest"] for w, _, _, d, e in call if w == "x" and d == core)
             g.tensor.wait_ge(T.sem["in%d" % j], n_in)
             mm = g.tensor.matmul(T.ps[:], T.ws[:], _hlf(T.land, j, h), start=(k == 0), stop=(k == N - 1))
         mm.then_inc(T.sem.mm, 1)

from concourse.bass import DstId, RemoteDMATransfer

N = 6
F = 128
HF = F // 2

SCRATCH = {
    "xs": ("sbuf", [128, N * F], "float32"),
    "ws": ("sbuf", [128, F], "float32"),
    "land": ("sbuf", [128, N * F], "float32"),
    "zs": ("sbuf", [128, HF], "float32"),
    "ps": ("psum", [128, HF], "float32"),
}
SEMAPHORES = (["ld_a0", "ld_a1", "ld_b", "ld_w", "rl", "inw", "mm", "zr", "st_a", "st_b", "sent"]
              + ["in%d" % j for j in range(N)] + ["got%d" % j for j in range(N)])


def _bits(mask):
    return [e for e in range(mask.bit_length()) if (mask >> e) & 1]


def _mask(engines):
    m = 0
    for e in engines:
        m |= 1 << e
    return m


def _split(engines, k):
    if k == 1:
        return [engines]
    return _split(engines[0::2], k // 2) + _split(engines[1::2], k - k // 2)


def _runs(blocks):
    runs = []
    for r in sorted(blocks):
        if runs and runs[-1][1] == r:
            runs[-1] = (runs[-1][0], r + 1)
        else:
            runs.append((r, r + 1))
    runs.sort(key=lambda ab: ab[0] - ab[1])
    return runs


def _blk(t, r):
    return t[:, r * F:(r + 1) * F]


def _hlf(t, r, h):
    return t[:, r * F + h * HF:r * F + (h + 1) * HF]


def _plan(T, topo):
    ranks = list(T.cores)
    p = {"ranks": ranks, "direct": [], "cross": [], "relay": [], "H": [], "waves": [], "late": []}
    for i, c in enumerate(ranks):
        others = [r for r in range(N) if r != i]
        direct = [r for r in others if topo.may_write(c, ranks[r])]
        cross = [r for r in others if not topo.may_write(c, ranks[r])]
        chipmates = [d for d in range(c - topo.CORES_PER_CHIP, c + topo.CORES_PER_CHIP)
                     if d != c and d >= 0 and topo.host(d) == topo.host(c) and topo.chip(d) == topo.chip(c)]
        owners = [d for d in chipmates if all(topo.may_write(d, ranks[r]) for r in others)]
        near = [d for d in owners if topo.die(d) == topo.die(c)]
        far = [d for d in owners if topo.die(d) != topo.die(c)]
        seq = []
        for a, b in zip(near, far):
            seq += [a, b]
        place = sorted(direct + [i]).index(i)
        m = len(cross)
        p["direct"].append(direct)
        p["cross"].append(cross)
        p["relay"].append({r: seq[(q + place) % m] for q, r in enumerate(cross)})
        p["H"].append(seq[0:2])
        inner = cross[m // 4:m // 4 + m // 2]
        outer = [r for r in cross if r not in inner]
        k = (2 * place // (len(direct) + 1)) % 2
        p["waves"].append([inner, outer] if k == 0 else [outer, inner])
        plane = sorted(direct + [i])
        p["late"].append(plane[(place + 1) % len(plane)])
    return p


def _rank_calls(p, i, topo):
    c = p["ranks"][i]
    hs = p["H"][i]
    on = _bits(topo.mask(c, hs[0]))
    off = on
    for r in p["direct"][i]:
        off = [e for e in off if e in _bits(topo.mask(c, p["H"][r][0]))]
    extra = [e for e in on if e not in off]
    pool = on if 4 * len(p["cross"][i]) > len(extra) else extra
    waves = []
    for wave in p["waves"][i]:
        jobs = sorted([(r, p["relay"][i][r]) for r in wave], key=lambda rd: (topo.die(rd[1]) != topo.die(c), rd[0]))
        waves.append([("x", r, None, d, e) for (r, d), e in zip(jobs, _split(pool, len(jobs)))])
    dl = [r for r in p["direct"][i] if r != p["late"][i]] + [p["late"][i]]
    away = [(r, h) for r in dl for h in range(2)]
    n1 = 1
    while 2 * n1 <= len(away):
        n1 *= 2
    first = [("x", r, h, p["H"][r][h], e) for (r, h), e in zip(away[:n1], _split(off, n1))]
    own = [("x", i, h, hs[h], e) for h, e in zip(range(2), _split(extra, 2))]
    if n1 < len(away):
        more = [("x", r, h, p["H"][r][h], e) for (r, h), e in zip(away[n1:], _split(off, len(away) - n1))]
        wh = [("wh", i, k, hs[h], e) for (k, h), e in zip([(k, h) for k in range(2) for h in range(2)], _split(extra, 4))]
        rest = [(["ld_w", "ld_b"], first + wh), ([], more + own)]
    else:
        rest = [(["ld_w"], [("w", i, None, hs[h], e) for h, e in zip(range(2), _split(extra, 2))]), (["ld_b"], first + own)]
    return {"waves": waves, "rest": rest}


def rank_program(g, core, T, topo):
    p = _plan(T, topo)
    ranks, H = p["ranks"], p["H"]
    calls = [_rank_calls(p, j, topo) for j in range(N)]
    got = lambda r: T.sem["got%d" % r]
    back_on = lambda r, h: _split([e for e in _bits(topo.mask(H[r][h], ranks[r]))
                                   if e not in _bits(topo.mask(H[r][h], ranks[(r + 1) % N]))], 2)[0]
    back_off = lambda r, h: _bits(min(topo.mask(H[r][h], ranks[d]) for d in range(N) if d != r))

    def dst_id(d):
        rid, pid = topo.addr(d, core)
        return DstId(rid=rid, pnc=pid)

    i = T.rank_of(core)
    if i is not None:
        rest = [r for r in range(N) if r not in p["cross"][i]]
        loads = {"ld_a0": _runs(p["waves"][i][0]), "ld_a1": _runs(p["waves"][i][1]), "ld_w": [None], "ld_b": _runs(rest)}
        queues = [g.sync, g.scalar]
        load = [0, 0]
        for name in ("ld_a0", "ld_a1", "ld_w", "ld_b"):
            for run in loads[name]:
                k = 0 if load[0] <= load[1] else 1
                if run is None:
                    queues[k].dma_start(T.ws[:], T.w[:]).then_inc(T.sem[name], 16)
                    load[k] += 1
                else:
                    a, b = run
                    queues[k].dma_start(T.xs[:, a * F:b * F], T.x[:, a * F:b * F]).then_inc(T.sem[name], 16)
                    load[k] += b - a
        sent = 0
        for names, call in [(["ld_a0"], calls[i]["waves"][0]), (["ld_a1"], calls[i]["waves"][1])] + calls[i]["rest"]:
            for name in names:
                g.wait_ge(T.sem[name], 16 * len(loads[name]))
            trs = []
            for what, r, h, d, eng in call:
                if what == "w":
                    src, dst, rs = T.ws[:], T.ws[:], T.sem.inw
                elif what == "wh":
                    src, dst, rs = _hlf(T.ws, 0, h), _hlf(T.ws, 0, h), T.sem.inw
                elif h is None:
                    src, dst, rs = _blk(T.xs, r), _blk(T.xs, r), T.sem.rl
                else:
                    src, dst, rs = _hlf(T.xs, r, h), _hlf(T.land, i, h), T.sem["in%d" % i]
                trs.append(RemoteDMATransfer(dst_ids=[dst_id(d)], dma_engine_mask=_mask(eng), remote_sem=rs,
                                             src=src, dst=dst))
                sent += len(eng)
            g.remote_dma_fused(trs, local_sem=T.sem.sent)
        turn = sorted(range(N), key=lambda r: (i - r) % N)
        for q, ss, mine in ((g.sync, T.sem.st_a, turn[0::2]), (g.scalar, T.sem.st_b, turn[1::2])):
            for r in mine:
                q.wait_ge(got(r), sum(len(back_on(r, h)) if r == i else len(back_off(r, h)) for h in range(2)))
                q.dma_start(_blk(T.y, r), _blk(T.land, r)).then_inc(ss, 16)
            q.wait_ge(ss, 16 * len(mine))
        g.wait_ge(T.sem.sent, sent)
        return

    relay_eng = lambda d, r: _split(_bits(min(topo.mask(d, H[r][h]) for h in range(2))), 2)
    sent = 0
    for j in range(N):
        for call in calls[j]["waves"]:
            for what, r, _h, d, eng in call:
                if d == core:
                    g.wait_ge(T.sem.rl, len(eng))
                    es = relay_eng(core, r)
                    g.remote_dma_fused([RemoteDMATransfer(dst_ids=[dst_id(H[r][h])], dma_engine_mask=_mask(es[h]),
                                                          remote_sem=T.sem["in%d" % j], src=_hlf(T.xs, r, h),
                                                          dst=_hlf(T.land, j, h)) for h in range(2)],
                                       local_sem=T.sem.sent)
                    sent += sum(len(e) for e in es)

    mine = [(r, h) for r in range(N) for h in range(2) if H[r][h] == core]
    for r, h in mine:
        two = lambda j: any(w == "wh" for _, call in calls[j]["rest"] for w, _, _, _, _ in call)
        last = [j for j in p["direct"][r] if two(j) and p["late"][j] == r]
        soon = [j for j in p["direct"][r] if j not in last]
        order = ((soon + [r] if two(r) else [r] + soon) + [j for j in p["cross"][r] if r in p["waves"][j][0]]
                 + last + [j for j in p["cross"][r] if r not in p["waves"][j][0]])
        g.tensor.wait_ge(T.sem.inw, sum(len(e) for _, call in calls[r]["rest"] for w, _, _, d, e in call
                                        if w != "x" and d == core))
        for k, j in enumerate(order):
            if j in p["cross"][r]:
                n_in = len(relay_eng(p["relay"][j][r], r)[h])
            else:
                n_in = sum(len(e) for _, call in calls[j]["rest"] for w, _, _, d, e in call if w == "x" and d == core)
            g.tensor.wait_ge(T.sem["in%d" % j], n_in)
            mm = g.tensor.matmul(T.ps[:], T.ws[:], _hlf(T.land, j, h), start=(k == 0), stop=(k == N - 1))
        mm.then_inc(T.sem.mm, 1)
        g.vector.wait_ge(T.sem.mm, 1)
        g.vector.tensor_copy(T.zs[:], T.ps[:]).then_inc(T.sem.zr, 1)
        g.wait_ge(T.sem.zr, 1)
        away = [(r + k) % N for k in range(1, N)]
        eng = back_off(r, h)
        g.remote_dma_fused([RemoteDMATransfer(dst_ids=[dst_id(ranks[d]) for d in away], dma_engine_mask=_mask(eng),
                                              remote_sem=got(r), srcs=[T.zs[:]], dsts=[_hlf(T.land, r, h) for d in away])],
                           local_sem=T.sem.sent)
        sent += len(eng)
        rid, pid = topo.addr(ranks[r], core)
        eng = back_on(r, h)
        g.remote_dma(out_ap=_hlf(T.land, r, h), in_ap=T.zs[:], remote_sem=got(r), local_sem=T.sem.sent, pid=pid,
                     routing_id=rid, dma_engine_mask=_mask(eng))
        sent += len(eng)
    if sent:
        g.wait_ge(T.sem.sent, sent)
